import numpy as np
import ml_dtypes


def mxq(x, axis, fmt="e4m3"):
    dtype, down = {"e4m3": (ml_dtypes.float8_e4m3fn, 7), "e5m2": (ml_dtypes.float8_e5m2, 14)}[fmt]
    v = np.moveaxis(np.asarray(x, np.float32).astype(ml_dtypes.bfloat16).astype(np.float64), axis, -1)
    blocks = v.reshape(v.shape[:-1] + (-1, 32))
    amax = np.abs(blocks).max(-1, keepdims=True)
    byte = np.maximum(np.where(amax > 0, np.frexp(amax)[1] - 1 + 127, 0) - down, 1)
    scale = np.exp2(byte - 127.0)
    codes = (blocks / scale).astype(np.float32).astype(dtype).astype(np.float64)
    return np.moveaxis((codes * scale).reshape(v.shape), -1, axis)


WIDE = False


def mx_kscale(k):
    if not WIDE:
        return np.ones(k)
    levels = np.array([10, -10, 5, -5, 0])
    if k % 512:
        return np.exp2(np.random.permutation(np.resize(levels, k // 32))).repeat(32)
    a = np.empty((k // 512, 16))
    for p in range(k // 512):
        a[p, :8] = np.random.permutation(np.resize(levels, 8))
        for g in range(8):
            far = levels[np.abs(levels - a[p, g]) >= 10]
            a[p, g + 8] = far[np.random.randint(len(far))]
    return np.exp2(a.ravel()).repeat(32)


def f64(x):
    return np.asarray(x).astype(np.float64)


def striped(idx):
    return np.tile(idx.reshape(-1, 16).T, (8, 1)).astype(np.uint16)


def unstriped(offs):
    return offs[:16].T.reshape(-1).astype(np.int64)


def striped8(idx):
    return np.concatenate([x.reshape(-1, 16).T for x in idx]).astype(np.uint16)


def runs(offs, k):
    lists = np.stack([offs[16 * r : 16 * r + 16].T.reshape(-1) for r in range(8)]).astype(np.int64)
    return lists[np.arange(k) % 512 // 64]


def pack_weight(w):
    k, n = w.shape
    w = f64(np.asarray(w, np.float32).astype(ml_dtypes.bfloat16)).reshape(k // 32, 32, n)
    amax = np.abs(w).max(1)
    byte = np.clip(np.where(amax > 0, np.frexp(amax)[1] - 1 + 127 - 7, 1), 1, 254)
    scaled = (w * np.exp2(127.0 - byte)[:, None, :]).reshape(k, n).astype(np.float32)
    words = np.ascontiguousarray(scaled.reshape(k // 512, 128, 4, n).transpose(0, 1, 3, 2)).astype(ml_dtypes.float8_e4m3fn).view(np.uint8)
    return words, np.ascontiguousarray(byte.astype(np.uint8).reshape(k // 512, 16, n))


def unpack_weight(words, scales):
    g, p, n, _ = words.shape
    vals = np.ascontiguousarray(words).view(ml_dtypes.float8_e4m3fn).astype(np.float64) * np.repeat(np.exp2(scales.astype(np.float64) - 127.0), 8, axis=1)[..., None]
    return vals.transpose(0, 1, 3, 2).reshape(g * 512, n)


K, T, S, N, H = 512, 2048, 512, 512, 512


def setup_inputs():
    n = np.random.standard_normal
    s = mx_kscale(K)[:, None]
    u = mx_kscale(H)
    packed_xT = pack_weight(n((K, T)) * s)
    return {
        "x_words": packed_xT[0],
        "x_scales": packed_xT[1],
        "w1": (n((K, H)) / np.sqrt(K) / s).astype(np.float32),
        "cst": np.random.uniform(0.0, 1.5, (H, S)).astype(np.float32),
        "gn": (np.random.uniform(0.5, 1.5, (H, 1)) * u[:, None]).astype(np.float32),
        "w2": (n((H, N)) / np.sqrt(H) / u[:, None]).astype(np.float32),
        "res": (2 * n((N, S))).astype(np.float32),
        "offs": striped(np.random.permutation(T)[:S]),
        "di": striped8(np.stack([np.random.permutation(S) for _ in range(8)])),
        "dj": striped8(np.stack([np.random.permutation(S) for _ in range(8)])),
        "dk": striped8(np.stack([np.random.permutation(S) for _ in range(8)])),
    }


def reference(x_words, x_scales, w1, cst, gn, w2, res, offs, di, dj, dk):
    xq = unpack_weight(x_words, x_scales)[:, unstriped(offs)]
    y = mxq(f64(w1), 0, "e4m3").T @ xq
    z = f64(gn) * (f64(cst) - (np.log(np.exp(-1.0 * (y[np.arange(H)[:, None], runs(di, H)])) + np.exp(-1.0 * (y[np.arange(H)[:, None], runs(dj, H)])) + np.exp(-1.0 * (y[np.arange(H)[:, None], runs(dk, H)])))))
    return f64(res) + (mxq(f64(w2), 0, "e4m3").T @ mxq(z, 0, "e4m3"))

@@ -1,0 +1,208 @@
+from contextlib import ExitStack
+
+import concourse.mybir as mybir
+from concourse.masks import make_identity
+
+K, T, S, H, N = 512, 2048, 512, 512, 512
+FLOPS = 2 * K * H * S + 2 * H * N * S
+
+F32 = mybir.dt.float32
+BF16 = mybir.dt.bfloat16
+I32 = mybir.dt.int32
+U32 = mybir.dt.uint32
+U16 = mybir.dt.uint16
+U8 = mybir.dt.uint8
+FP8X4 = mybir.dt.float8_e4m3fn_x4
+ALU = mybir.AluOpType
+ACT = mybir.ActivationFunctionType
+
+P = 128
+PACK = 4
+BLOCK = 128
+CHUNK = 256
+HALF = S // 2
+CAP = 32.0
+W1_SPLIT = 52
+
+
+def tile_picked_softdtw_none_p_kernel(tc, x_words, x_scales, w1, cst, gn, w2, res, offs, di, dj, dk, out):
+    nc = tc.nc
+    with ExitStack() as ctx:
+        keep = ctx.enter_context(tc.tile_pool(name="keep", bufs=1))
+        work = ctx.enter_context(tc.tile_pool(name="work", bufs=2))
+        psum = ctx.enter_context(tc.psum_pool(name="psum", bufs=2))
+
+        offs_sb = keep.tile([P, S // 16], U16, name="offs_sb")
+        di_sb = keep.tile([P, S // 16], U16, name="di_sb")
+        dj_sb = keep.tile([P, S // 16], U16, name="dj_sb")
+        dk_sb = keep.tile([P, S // 16], U16, name="dk_sb")
+        w1_raw = keep.tile([P, PACK, H], F32, name="w1_raw")
+        w2_raw = keep.tile([P, PACK, N], F32, name="w2_raw")
+        words = keep.tile([P, T], I32, name="words", align_bytes=64)
+        scales = keep.tile([P, T], U8, name="scales", align_bytes=64)
+        cst_sb = keep.tile([P, PACK, S], F32, name="cst_sb")
+        res_sb = keep.tile([P, N // P, S], F32, name="res_sb")
+        gn_sb = keep.tile([P, PACK], F32, name="gn_sb")
+        ident = keep.tile([P, P], F32, name="ident")
+
+        nc.gpsimd.memset(scales[:].bitcast(I32), 0)
+        nc.sync.dma_start(offs_sb[:], offs)
+        nc.sync.dma_start(w1_raw[:], w1.rearrange("(p j) c -> p j c", j=PACK))
+        for q in range(4):
+            nc.sync.dma_start(scales[32 * q : 32 * q + 4, :].bitcast(I32), x_scales[0, 4 * q : 4 * q + 4, :].bitcast(I32))
+        nc.sync.dma_start(words[:], x_words[0].rearrange("p n t -> p (n t)").bitcast(I32))
+        nc.sync.dma_start(di_sb[:], di)
+        nc.sync.dma_start(dj_sb[:], dj)
+        nc.sync.dma_start(dk_sb[:], dk)
+        nc.sync.dma_start(cst_sb[:], cst.rearrange("(p t) j -> p t j", t=PACK))
+        nc.sync.dma_start(w2_raw[:], w2.rearrange("(p j) c -> p j c", j=PACK))
+        nc.sync.dma_start(gn_sb[:], gn.rearrange("(p t) o -> p (t o)", t=PACK))
+        nc.sync.dma_start(res_sb[:], res.rearrange("(m p) j -> p m j", p=P))
+        make_identity(nc, ident[:])
+
+        x_codes = keep.tile([P, S], U32, name="x_codes", align_bytes=64)
+        x_bytes = keep.tile([P, S], U8, name="x_bytes", align_bytes=64)
+        nc.vector.tensor_copy(x_bytes[:], scales[:].indirect(offs_sb[:]))
+
+        w1_bf = keep.tile([P, PACK * H], BF16, name="w1_bf", align_bytes=64)
+        dealt = w1_bf[:].rearrange("p (t m j) -> p m j t", t=PACK, j=PACK)
+        source = w1_raw[:].rearrange("p j (m t) -> p m j t", t=PACK)
+        nc.vector.tensor_copy(dealt[:, :W1_SPLIT], source[:, :W1_SPLIT])
+        nc.scalar.copy(dealt[:, W1_SPLIT:], source[:, W1_SPLIT:])
+        w1_codes = keep.tile([P, H], U32, name="w1_codes", align_bytes=64)
+        w1_bytes = keep.tile([P, H], U8, name="w1_bytes", align_bytes=64)
+        nc.vector.quantize_mx(out=w1_codes[:].bitcast(FP8X4), scales=w1_bytes[:], in_=w1_bf[:])
+
+        roles = ("sums", "base", "back", "acc")
+        banks = [[psum.tile([P, HALF], F32, name=f"y_bank{t}_{h}", tag=roles[t]) for h in range(2)] for t in range(PACK)]
+        y = [keep.tile([P, S], F32, name=f"y{t}") for t in range(PACK)]
+        halves = [slice(h * HALF, (h + 1) * HALF) for h in range(2)]
+        for h in range(2):
+            nc.vector.tensor_copy(x_codes[:, halves[h]], words[:].bitcast(U32).indirect(offs_sb[:, 16 * h : 16 * h + 16]))
+        for t in range(PACK):
+            for h in range(2):
+                nc.tensor.matmul_mx(
+                    out=banks[t][h][:],
+                    lhsT=w1_codes[:, t * P : (t + 1) * P].bitcast(FP8X4),
+                    lhsT_scale=w1_bytes[:, t * P : (t + 1) * P],
+                    rhs=x_codes[:, halves[h]].bitcast(FP8X4),
+                    rhs_scale=x_bytes[:, halves[h]],
+                    start=True,
+                    stop=True,
+                )
+                nc.scalar.copy(y[t][:, halves[h]], banks[t][h][:])
+
+        w2_bf = keep.tile([P, PACK * N], BF16, name="w2_bf", align_bytes=64)
+        nc.scalar.copy(
+            w2_bf[:].rearrange("p (c i j) -> p c j i", i=4, j=PACK),
+            w2_raw[:].rearrange("p j (c i) -> p c j i", i=4),
+        )
+        w2_codes = keep.tile([P, N], U32, name="w2_codes", align_bytes=64)
+        w2_bytes = keep.tile([P, N], U8, name="w2_bytes", align_bytes=64)
+
+        def turn(bank, src, col0, first, last):
+            for t in range(PACK):
+                nc.tensor.matmul(
+                    bank[:, t * P : (t + 1) * P], src[:, t, col0 : col0 + BLOCK], ident[:],
+                    start=first and t == 0, stop=last and t == PACK - 1, is_transpose=True,
+                )
+
+        def turn_back(bank, src, first, last):
+            for t in range(PACK):
+                nc.tensor.matmul(
+                    bank[:, t * P : (t + 1) * P], src[:, t * P : (t + 1) * P], ident[:],
+                    start=first and t == 0, stop=last and t == PACK - 1, is_transpose=True,
+                )
+
+        def look_up(c):
+            lists = slice(c * CHUNK // 16, (c + 1) * CHUNK // 16)
+            blocks = range(CHUNK // BLOCK)
+            a = work.tile([P, PACK, CHUNK], F32, name="a")
+            d1 = work.tile([P, PACK, CHUNK], F32, name="d1")
+            m1 = work.tile([P, PACK, CHUNK], F32, name="m1")
+            d2 = work.tile([P, PACK, CHUNK], F32, name="d2")
+            q = work.tile([P, PACK, CHUNK], F32, name="q")
+            mag = keep.tile([P, PACK, CHUNK], F32, name="mag", tag="held")
+            e1 = work.tile([P, PACK, CHUNK], F32, name="e1")
+            e2 = keep.tile([P, PACK, CHUNK], F32, name="e2", tag="late", align_bytes=64)
+            for t in range(PACK):
+                nc.vector.tensor_copy(a[:, t, :], y[t][:].indirect(di_sb[:, lists]))
+            for t in range(PACK):
+                nc.vector.tensor_tensor(d1[:, t, :], y[t][:].indirect(dj_sb[:, lists]), a[:, t, :], ALU.subtract)
+            for h in range(2):
+                nc.vector.scalar_tensor_tensor(m1[:, 2 * h : 2 * h + 2, :], d1[:, 2 * h : 2 * h + 2, :], 0.0, a[:, 2 * h : 2 * h + 2, :], ALU.min, ALU.add)
+            nc.scalar.activation(mag[:], d1[:], ACT.Abs)
+            nc.scalar.activation(e1[:], mag[:], ACT.Exp, scale=-1.0)
+            sums = [psum.tile([P, PACK * P], F32, name="sums", tag="sums") for b in blocks]
+            base = [psum.tile([P, PACK * P], F32, name="base", tag="base") for b in blocks]
+            for b in blocks:
+                turn(base[b], cst_sb, c * CHUNK + b * BLOCK, True, False)
+                turn(base[b], m1, b * BLOCK, False, False)
+            for b in blocks:
+                turn(sums[b], e1, b * BLOCK, True, False)
+            for t in range(PACK):
+                nc.vector.tensor_tensor(d2[:, t, :], y[t][:].indirect(dk_sb[:, lists]), m1[:, t, :], ALU.subtract)
+            for h in range(2):
+                nc.vector.tensor_scalar(q[:, 2 * h : 2 * h + 2, :], d2[:, 2 * h : 2 * h + 2, :], -CAP, -1.0, ALU.max, ALU.mult)
+            nc.scalar.activation(e2[:], q[:], ACT.Exp)
+            for b in blocks:
+                turn(base[b], d2, b * BLOCK, False, False)
+            for b in blocks:
+                turn(sums[b], e2, b * BLOCK, False, True)
+                turn(base[b], q, b * BLOCK, False, True)
+            return sums, base
+
+        def logarithms(sums, base):
+            backs = []
+            for b in range(len(sums)):
+                if b == len(sums) - 1:
+                    logs = keep.tile([P, PACK * P], F32, name="logs_last", tag="held")
+                else:
+                    logs = work.tile([P, PACK * P], F32, name="logs")
+                rest = work.tile([P, PACK * P], F32, name="rest")
+                back = psum.tile([P, PACK * P], F32, name="back", tag="back")
+                nc.scalar.activation(logs[:], sums[b][:], ACT.Ln, bias=1.0)
+                nc.scalar.activation(rest[:], base[b][:], ACT.Copy, scale=-1.0)
+                turn_back(back, logs, True, False)
+                turn_back(back, rest, False, True)
+                backs.append(back)
+            return backs
+
+        def finish(c, backs):
+            for b, back in enumerate(backs):
+                cols = slice(c * CHUNK + b * BLOCK, c * CHUNK + (b + 1) * BLOCK)
+                z_bf = work.tile([P, BLOCK * PACK], BF16, name="z_bf", align_bytes=64)
+                nc.vector.scalar_tensor_tensor(
+                    z_bf[:].rearrange("p (j t) -> p j t", t=PACK),
+                    back[:].rearrange("p (t j) -> p j t", t=PACK),
+                    -1.0,
+                    gn_sb[:].unsqueeze(1).to_broadcast([P, BLOCK, PACK]),
+                    ALU.mult,
+                    ALU.mult,
+                )
+                if c == 0 and b == 0:
+                    z_codes = keep.tile([P, BLOCK], U32, name="z_codes_first", tag="late", align_bytes=64)
+                else:
+                    z_codes = work.tile([P, BLOCK], U32, name="z_codes", align_bytes=64)
+                z_bytes = work.tile([P, BLOCK], U8, name="z_bytes", align_bytes=64)
+                nc.vector.quantize_mx(out=z_codes[:].bitcast(FP8X4), scales=z_bytes[:], in_=z_bf[:])
+                acc = psum.tile([P, N // P, BLOCK], F32, name="acc", tag="acc")
+                for m in range(N // P):
+                    nc.tensor.matmul_mx(
+                        out=acc[:, m, :],
+                        lhsT=w2_codes[:, m * P : (m + 1) * P].bitcast(FP8X4),
+                        lhsT_scale=w2_bytes[:, m * P : (m + 1) * P],
+                        rhs=z_codes[:].bitcast(FP8X4),
+                        rhs_scale=z_bytes[:],
+                        start=True,
+                        stop=True,
+                    )
+                total = work.tile([P, N // P, BLOCK], F32, name="total")
+                nc.vector.tensor_tensor(total[:], acc[:], res_sb[:, :, cols], ALU.add)
+                nc.sync.dma_start(out.rearrange("(m p) j -> p m j", p=P)[:, :, cols], total[:])
+
+        first = logarithms(*look_up(0))
+        second = look_up(1)
+        nc.vector.quantize_mx(out=w2_codes[:].bitcast(FP8X4), scales=w2_bytes[:], in_=w2_bf[:])
+        finish(0, first)
+        finish(1, logarithms(*second))

@@ -22,6 +22,8 @@ BLOCK = 128
 CHUNK = 256
 HALF = S // 2
 CAP = 32.0
+SUM, LINEAR = 0, 1
+BANK = 512
 W1_SPLIT = 52
 
 
@@ -30,14 +32,15 @@ def tile_picked_softdtw_none_p_kernel(tc, x_words, x_scales, w1, cst, gn, w2, re
     with ExitStack() as ctx:
         keep = ctx.enter_context(tc.tile_pool(name="keep", bufs=1))
         work = ctx.enter_context(tc.tile_pool(name="work", bufs=2))
-        psum = ctx.enter_context(tc.psum_pool(name="psum", bufs=2))
+        stores = ctx.enter_context(tc.tile_pool(name="stores", bufs=4))
+        psum = ctx.enter_context(tc.psum_pool(name="psum", bufs=1))
 
         offs_sb = keep.tile([P, S // 16], U16, name="offs_sb")
         di_sb = keep.tile([P, S // 16], U16, name="di_sb")
         dj_sb = keep.tile([P, S // 16], U16, name="dj_sb")
         dk_sb = keep.tile([P, S // 16], U16, name="dk_sb")
         w1_raw = keep.tile([P, PACK, H], F32, name="w1_raw")
-        w2_raw = keep.tile([P, PACK, N], F32, name="w2_raw")
+        w2_raw = keep.tile([P, PACK, N], F32, name="w2_raw", tag="late0", align_bytes=64)
         words = keep.tile([P, T], I32, name="words", align_bytes=64)
         scales = keep.tile([P, T], U8, name="scales", align_bytes=64)
         cst_sb = keep.tile([P, PACK, S], F32, name="cst_sb")
@@ -54,8 +57,8 @@ def tile_picked_softdtw_none_p_kernel(tc, x_words, x_scales, w1, cst, gn, w2, re
         nc.sync.dma_start(di_sb[:], di)
         nc.sync.dma_start(dj_sb[:], dj)
         nc.sync.dma_start(dk_sb[:], dk)
-        nc.sync.dma_start(cst_sb[:], cst.rearrange("(p t) j -> p t j", t=PACK))
         nc.sync.dma_start(w2_raw[:], w2.rearrange("(p j) c -> p j c", j=PACK))
+        nc.sync.dma_start(cst_sb[:], cst.rearrange("(p t) j -> p t j", t=PACK))
         nc.sync.dma_start(gn_sb[:], gn.rearrange("(p t) o -> p (t o)", t=PACK))
         nc.sync.dma_start(res_sb[:], res.rearrange("(m p) j -> p m j", p=P))
         make_identity(nc, ident[:])
@@ -69,12 +72,12 @@ def tile_picked_softdtw_none_p_kernel(tc, x_words, x_scales, w1, cst, gn, w2, re
         source = w1_raw[:].rearrange("p j (m t) -> p m j t", t=PACK)
         nc.vector.tensor_copy(dealt[:, :W1_SPLIT], source[:, :W1_SPLIT])
         nc.scalar.copy(dealt[:, W1_SPLIT:], source[:, W1_SPLIT:])
-        w1_codes = keep.tile([P, H], U32, name="w1_codes", align_bytes=64)
+        w1_codes = keep.tile([P, H], U32, name="w1_codes", tag="weights", align_bytes=64)
         w1_bytes = keep.tile([P, H], U8, name="w1_bytes", align_bytes=64)
         nc.vector.quantize_mx(out=w1_codes[:].bitcast(FP8X4), scales=w1_bytes[:], in_=w1_bf[:])
 
-        roles = ("sums", "base", "back", "acc")
-        banks = [[psum.tile([P, HALF], F32, name=f"y_bank{t}_{h}", tag=roles[t]) for h in range(2)] for t in range(PACK)]
+        roles = ("turned0", "turned1", "turned2", "turned3", "back0", "back1", "acc0", "acc1")
+        banks = [[psum.tile([P, HALF], F32, name=f"y_bank{t}_{h}", tag=roles[2 * t + h]) for h in range(2)] for t in range(PACK)]
         y = [keep.tile([P, S], F32, name=f"y{t}") for t in range(PACK)]
         halves = [slice(h * HALF, (h + 1) * HALF) for h in range(2)]
         for h in range(2):
@@ -92,19 +95,19 @@ def tile_picked_softdtw_none_p_kernel(tc, x_words, x_scales, w1, cst, gn, w2, re
                 )
                 nc.scalar.copy(y[t][:, halves[h]], banks[t][h][:])
 
-        w2_bf = keep.tile([P, PACK * N], BF16, name="w2_bf", align_bytes=64)
+        w2_bf = keep.tile([P, PACK * N], BF16, name="w2_bf", tag="weights", align_bytes=64)
         nc.scalar.copy(
             w2_bf[:].rearrange("p (c i j) -> p c j i", i=4, j=PACK),
             w2_raw[:].rearrange("p j (c i) -> p c j i", i=4),
         )
-        w2_codes = keep.tile([P, N], U32, name="w2_codes", align_bytes=64)
         w2_bytes = keep.tile([P, N], U8, name="w2_bytes", align_bytes=64)
 
-        def turn(bank, src, col0, first, last):
+        def turn(pair, region, src, col0, first, last):
             for t in range(PACK):
+                at = region * HALF + (t % 2) * P
                 nc.tensor.matmul(
-                    bank[:, t * P : (t + 1) * P], src[:, t, col0 : col0 + BLOCK], ident[:],
-                    start=first and t == 0, stop=last and t == PACK - 1, is_transpose=True,
+                    pair[t // 2][:, at : at + P], src[:, t, col0 : col0 + BLOCK], ident[:],
+                    start=first and t % 2 == 0, stop=last and t % 2 == 1, is_transpose=True,
                 )
 
         def turn_back(bank, src, first, last):
@@ -117,79 +120,81 @@ def tile_picked_softdtw_none_p_kernel(tc, x_words, x_scales, w1, cst, gn, w2, re
         def look_up(c):
             lists = slice(c * CHUNK // 16, (c + 1) * CHUNK // 16)
             blocks = range(CHUNK // BLOCK)
-            a = work.tile([P, PACK, CHUNK], F32, name="a")
-            d1 = work.tile([P, PACK, CHUNK], F32, name="d1")
-            m1 = work.tile([P, PACK, CHUNK], F32, name="m1")
+            a = keep.tile([P, PACK, CHUNK], F32, name="a", tag=f"pair{c}", align_bytes=64)
+            d1 = keep.tile([P, PACK, CHUNK], F32, name="d1", tag="d1")
+            m1 = keep.tile([P, PACK, CHUNK], F32, name="m1", tag=f"pair{1 - c}", align_bytes=64)
             d2 = work.tile([P, PACK, CHUNK], F32, name="d2")
-            q = work.tile([P, PACK, CHUNK], F32, name="q")
-            mag = keep.tile([P, PACK, CHUNK], F32, name="mag", tag="held")
-            e1 = work.tile([P, PACK, CHUNK], F32, name="e1")
-            e2 = keep.tile([P, PACK, CHUNK], F32, name="e2", tag="late", align_bytes=64)
+            q = keep.tile([P, PACK, CHUNK], F32, name="q", tag="q", align_bytes=64)
+            mag = [keep.tile([P, PACK, BLOCK], F32, name=f"mag{b}", tag=f"late{b}", align_bytes=64) for b in blocks]
+            e1 = [work.tile([P, PACK, BLOCK], F32, name=f"e1_{b}") for b in blocks]
             for t in range(PACK):
                 nc.vector.tensor_copy(a[:, t, :], y[t][:].indirect(di_sb[:, lists]))
             for t in range(PACK):
                 nc.vector.tensor_tensor(d1[:, t, :], y[t][:].indirect(dj_sb[:, lists]), a[:, t, :], ALU.subtract)
             for h in range(2):
                 nc.vector.scalar_tensor_tensor(m1[:, 2 * h : 2 * h + 2, :], d1[:, 2 * h : 2 * h + 2, :], 0.0, a[:, 2 * h : 2 * h + 2, :], ALU.min, ALU.add)
-            nc.scalar.activation(mag[:], d1[:], ACT.Abs)
-            nc.scalar.activation(e1[:], mag[:], ACT.Exp, scale=-1.0)
-            sums = [psum.tile([P, PACK * P], F32, name="sums", tag="sums") for b in blocks]
-            base = [psum.tile([P, PACK * P], F32, name="base", tag="base") for b in blocks]
             for b in blocks:
-                turn(base[b], cst_sb, c * CHUNK + b * BLOCK, True, False)
-                turn(base[b], m1, b * BLOCK, False, False)
+                nc.scalar.activation(mag[b][:], d1[:, :, b * BLOCK : (b + 1) * BLOCK], ACT.Abs)
             for b in blocks:
-                turn(sums[b], e1, b * BLOCK, True, False)
+                nc.scalar.activation(e1[b][:], mag[b][:], ACT.Exp, scale=-1.0)
+            pairs = [[psum.tile([P, 2 * HALF], F32, name="turned", tag=f"turned{2 * b + u}") for u in range(2)] for b in blocks]
+            for b in blocks:
+                turn(pairs[b], LINEAR, cst_sb, c * CHUNK + b * BLOCK, True, False)
+                turn(pairs[b], LINEAR, m1, b * BLOCK, False, False)
+            for b in blocks:
+                turn(pairs[b], SUM, e1[b], 0, False, False)
             for t in range(PACK):
                 nc.vector.tensor_tensor(d2[:, t, :], y[t][:].indirect(dk_sb[:, lists]), m1[:, t, :], ALU.subtract)
-            for h in range(2):
-                nc.vector.tensor_scalar(q[:, 2 * h : 2 * h + 2, :], d2[:, 2 * h : 2 * h + 2, :], -CAP, -1.0, ALU.max, ALU.mult)
-            nc.scalar.activation(e2[:], q[:], ACT.Exp)
             for b in blocks:
-                turn(base[b], d2, b * BLOCK, False, False)
+                nc.vector.tensor_scalar(q[:, :, b * BLOCK : (b + 1) * BLOCK], d2[:, :, b * BLOCK : (b + 1) * BLOCK], -CAP, -1.0, ALU.max, ALU.mult)
+            e2 = [keep.tile([P, PACK, BLOCK], F32, name=f"e2_{b}", tag=f"late{b}", align_bytes=64) for b in blocks]
             for b in blocks:
-                turn(sums[b], e2, b * BLOCK, False, True)
-                turn(base[b], q, b * BLOCK, False, True)
-            return sums, base
+                nc.scalar.activation(e2[b][:], q[:, :, b * BLOCK : (b + 1) * BLOCK], ACT.Exp)
+            for b in blocks:
+                turn(pairs[b], LINEAR, d2, b * BLOCK, False, False)
+            for b in blocks:
+                turn(pairs[b], LINEAR, q, b * BLOCK, False, False)
+            for b in blocks:
+                turn(pairs[b], SUM, e2[b], 0, False, True)
+            return pairs
 
-        def logarithms(sums, base):
-            backs = []
-            for b in range(len(sums)):
-                if b == len(sums) - 1:
-                    logs = keep.tile([P, PACK * P], F32, name="logs_last", tag="held")
+        def logarithms(pairs, steps):
+            backs = [psum.tile([P, PACK * P], F32, name="back", tag=f"back{b}") for b in range(len(pairs))]
+            for region, b in steps:
+                if region == SUM:
+                    part = keep.tile([P, PACK * P], F32, name=f"logs{b}", tag=f"late{b}", align_bytes=64)
                 else:
-                    logs = work.tile([P, PACK * P], F32, name="logs")
-                rest = work.tile([P, PACK * P], F32, name="rest")
-                back = psum.tile([P, PACK * P], F32, name="back", tag="back")
-                nc.scalar.activation(logs[:], sums[b][:], ACT.Ln, bias=1.0)
-                nc.scalar.activation(rest[:], base[b][:], ACT.Copy, scale=-1.0)
-                turn_back(back, logs, True, False)
-                turn_back(back, rest, False, True)
-                backs.append(back)
+                    part = work.tile([P, PACK * P], F32, name="rest")
+                for u in range(2):
+                    src = pairs[b][u][:, region * HALF : (region + 1) * HALF]
+                    if region == SUM:
+                        nc.scalar.activation(part[:, u * HALF : (u + 1) * HALF], src, ACT.Ln, bias=1.0)
+                    else:
+                        nc.scalar.activation(part[:, u * HALF : (u + 1) * HALF], src, ACT.Copy, scale=-1.0)
+                turn_back(backs[b], part, region == SUM, region == LINEAR)
             return backs
 
-        def finish(c, backs):
+        def finish(first, backs, z_codes):
+            width = len(backs) * BLOCK
+            cols = slice(first * BLOCK, first * BLOCK + width)
+            z_bf = work.tile([P, width * PACK], BF16, name="z_bf", align_bytes=64)
             for b, back in enumerate(backs):
-                cols = slice(c * CHUNK + b * BLOCK, c * CHUNK + (b + 1) * BLOCK)
-                z_bf = work.tile([P, BLOCK * PACK], BF16, name="z_bf", align_bytes=64)
                 nc.vector.scalar_tensor_tensor(
-                    z_bf[:].rearrange("p (j t) -> p j t", t=PACK),
+                    z_bf[:, b * BLOCK * PACK : (b + 1) * BLOCK * PACK].rearrange("p (j t) -> p j t", t=PACK),
                     back[:].rearrange("p (t j) -> p j t", t=PACK),
                     -1.0,
                     gn_sb[:].unsqueeze(1).to_broadcast([P, BLOCK, PACK]),
                     ALU.mult,
                     ALU.mult,
                 )
-                if c == 0 and b == 0:
-                    z_codes = keep.tile([P, BLOCK], U32, name="z_codes_first", tag="late", align_bytes=64)
-                else:
-                    z_codes = work.tile([P, BLOCK], U32, name="z_codes", align_bytes=64)
-                z_bytes = work.tile([P, BLOCK], U8, name="z_bytes", align_bytes=64)
-                nc.vector.quantize_mx(out=z_codes[:].bitcast(FP8X4), scales=z_bytes[:], in_=z_bf[:])
-                acc = psum.tile([P, N // P, BLOCK], F32, name="acc", tag="acc")
-                for m in range(N // P):
+            z_bytes = work.tile([P, width], U8, name="z_bytes", align_bytes=64)
+            nc.vector.quantize_mx(out=z_codes[:].bitcast(FP8X4), scales=z_bytes[:], in_=z_bf[:])
+            per_bank = BANK // width
+            for m0 in range(0, N // P, per_bank):
+                acc = psum.tile([P, per_bank, width], F32, name="acc", tag=f"acc{(first + m0 // per_bank) % 2}")
+                for m in range(m0, m0 + per_bank):
                     nc.tensor.matmul_mx(
-                        out=acc[:, m, :],
+                        out=acc[:, m - m0, :],
                         lhsT=w2_codes[:, m * P : (m + 1) * P].bitcast(FP8X4),
                         lhsT_scale=w2_bytes[:, m * P : (m + 1) * P],
                         rhs=z_codes[:].bitcast(FP8X4),
@@ -197,12 +202,15 @@ def tile_picked_softdtw_none_p_kernel(tc, x_words, x_scales, w1, cst, gn, w2, re
                         start=True,
                         stop=True,
                     )
-                total = work.tile([P, N // P, BLOCK], F32, name="total")
-                nc.vector.tensor_tensor(total[:], acc[:], res_sb[:, :, cols], ALU.add)
-                nc.sync.dma_start(out.rearrange("(m p) j -> p m j", p=P)[:, :, cols], total[:])
+                total = stores.tile([P, per_bank, width], F32, name="total")
+                nc.vector.tensor_tensor(total[:], acc[:], res_sb[:, m0 : m0 + per_bank, cols], ALU.add)
+                nc.sync.dma_start(out.rearrange("(m p) j -> p m j", p=P)[:, m0 : m0 + per_bank, cols], total[:])
 
-        first = logarithms(*look_up(0))
+        first = logarithms(look_up(0), ((SUM, 0), (SUM, 1), (LINEAR, 0), (LINEAR, 1)))
         second = look_up(1)
+        w2_codes = keep.tile([P, N], U32, name="w2_codes", tag="pair0", align_bytes=64)
         nc.vector.quantize_mx(out=w2_codes[:].bitcast(FP8X4), scales=w2_bytes[:], in_=w2_bf[:])
-        finish(0, first)
-        finish(1, logarithms(*second))
+        finish(0, first, keep.tile([P, CHUNK], U32, name="z_codes", tag="q", align_bytes=64))
+        last = logarithms(second, ((SUM, 0), (LINEAR, 0), (SUM, 1), (LINEAR, 1)))
+        for b, back in enumerate(last):
+            finish(2 + b, [back], work.tile([P, BLOCK], U32, name="z_codes_block", align_bytes=64))

@@ -23,7 +23,6 @@ CHUNK = 256
 HALF = S // 2
 CAP = 32.0
 SUM, LINEAR = 0, 1
-BANK = 512
 W1_SPLIT = 52
 
 
@@ -40,7 +39,7 @@ def tile_picked_softdtw_none_p_kernel(tc, x_words, x_scales, w1, cst, gn, w2, re
         dj_sb = keep.tile([P, S // 16], U16, name="dj_sb")
         dk_sb = keep.tile([P, S // 16], U16, name="dk_sb")
         w1_raw = keep.tile([P, PACK, H], F32, name="w1_raw")
-        w2_raw = keep.tile([P, PACK, N], F32, name="w2_raw", tag="late0", align_bytes=64)
+        w2_raw = [keep.tile([P, PACK, N // 2], F32, name="w2_raw", tag=f"late{h}", align_bytes=64) for h in range(2)]
         words = keep.tile([P, T], I32, name="words", align_bytes=64)
         scales = keep.tile([P, T], U8, name="scales", align_bytes=64)
         cst_sb = keep.tile([P, PACK, S], F32, name="cst_sb")
@@ -57,7 +56,8 @@ def tile_picked_softdtw_none_p_kernel(tc, x_words, x_scales, w1, cst, gn, w2, re
         nc.sync.dma_start(di_sb[:], di)
         nc.sync.dma_start(dj_sb[:], dj)
         nc.sync.dma_start(dk_sb[:], dk)
-        nc.sync.dma_start(w2_raw[:], w2.rearrange("(p j) c -> p j c", j=PACK))
+        for h in range(2):
+            nc.sync.dma_start(w2_raw[h][:], w2.rearrange("(p j) c -> p j c", j=PACK)[:, :, h * N // 2 : (h + 1) * N // 2])
         nc.sync.dma_start(cst_sb[:], cst.rearrange("(p t) j -> p t j", t=PACK))
         nc.sync.dma_start(gn_sb[:], gn.rearrange("(p t) o -> p (t o)", t=PACK))
         nc.sync.dma_start(res_sb[:], res.rearrange("(m p) j -> p m j", p=P))
@@ -76,34 +76,34 @@ def tile_picked_softdtw_none_p_kernel(tc, x_words, x_scales, w1, cst, gn, w2, re
         w1_bytes = keep.tile([P, H], U8, name="w1_bytes", align_bytes=64)
         nc.vector.quantize_mx(out=w1_codes[:].bitcast(FP8X4), scales=w1_bytes[:], in_=w1_bf[:])
 
-        roles = ("turned0", "turned1", "turned2", "turned3", "back0", "back1", "acc0", "acc1")
-        banks = [[psum.tile([P, HALF], F32, name=f"y_bank{t}_{h}", tag=roles[2 * t + h]) for h in range(2)] for t in range(PACK)]
         y = [keep.tile([P, S], F32, name=f"y{t}") for t in range(PACK)]
         halves = [slice(h * HALF, (h + 1) * HALF) for h in range(2)]
         for h in range(2):
             nc.vector.tensor_copy(x_codes[:, halves[h]], words[:].bitcast(U32).indirect(offs_sb[:, 16 * h : 16 * h + 16]))
-        for t in range(PACK):
-            for h in range(2):
-                nc.tensor.matmul_mx(
-                    out=banks[t][h][:],
-                    lhsT=w1_codes[:, t * P : (t + 1) * P].bitcast(FP8X4),
-                    lhsT_scale=w1_bytes[:, t * P : (t + 1) * P],
-                    rhs=x_codes[:, halves[h]].bitcast(FP8X4),
-                    rhs_scale=x_bytes[:, halves[h]],
-                    start=True,
-                    stop=True,
-                )
-                nc.scalar.copy(y[t][:, halves[h]], banks[t][h][:])
+        pieces = [(0, halves[0]), (0, halves[1])] + [(t, slice(0, S)) for t in range(1, PACK)]
+        for (t, cols), tag in zip(pieces, ("turned0", "turned1", "turned2", "turned3", "back0")):
+            bank = psum.tile([P, cols.stop - cols.start], F32, name="y_bank", tag=tag)
+            nc.tensor.matmul_mx(
+                out=bank[:],
+                lhsT=w1_codes[:, t * P : (t + 1) * P].bitcast(FP8X4),
+                lhsT_scale=w1_bytes[:, t * P : (t + 1) * P],
+                rhs=x_codes[:, cols].bitcast(FP8X4),
+                rhs_scale=x_bytes[:, cols],
+                start=True,
+                stop=True,
+            )
+            nc.scalar.copy(y[t][:, cols], bank[:])
 
         w2_bf = keep.tile([P, PACK * N], BF16, name="w2_bf", tag="weights", align_bytes=64)
-        nc.scalar.copy(
-            w2_bf[:].rearrange("p (c i j) -> p c j i", i=4, j=PACK),
-            w2_raw[:].rearrange("p j (c i) -> p c j i", i=4),
-        )
+        for h in range(2):
+            nc.scalar.copy(
+                w2_bf[:, h * 2 * N : (h + 1) * 2 * N].rearrange("p (c i j) -> p c j i", i=4, j=PACK),
+                w2_raw[h][:].rearrange("p j (c i) -> p c j i", i=4),
+            )
         w2_bytes = keep.tile([P, N], U8, name="w2_bytes", align_bytes=64)
 
-        def turn(pair, region, src, col0, first, last):
-            for t in range(PACK):
+        def turn(pair, region, src, col0, first, last, tiles=range(PACK)):
+            for t in tiles:
                 at = region * HALF + (t % 2) * P
                 nc.tensor.matmul(
                     pair[t // 2][:, at : at + P], src[:, t, col0 : col0 + BLOCK], ident[:],
@@ -150,11 +150,11 @@ def tile_picked_softdtw_none_p_kernel(tc, x_words, x_scales, w1, cst, gn, w2, re
             e2 = [keep.tile([P, PACK, BLOCK], F32, name=f"e2_{b}", tag=f"late{b}", align_bytes=64) for b in blocks]
             for b in blocks:
                 nc.scalar.activation(e2[b][:], q[:, :, b * BLOCK : (b + 1) * BLOCK], ACT.Exp)
-            for b in blocks:
-                turn(pairs[b], LINEAR, d2, b * BLOCK, False, False)
+            for half in ((0, 1), (2, 3)):
+                for b in blocks:
+                    turn(pairs[b], LINEAR, d2, b * BLOCK, False, False, half)
             for b in blocks:
                 turn(pairs[b], LINEAR, q, b * BLOCK, False, False)
-            for b in blocks:
                 turn(pairs[b], SUM, e2[b], 0, False, True)
             return pairs
 
@@ -174,7 +174,7 @@ def tile_picked_softdtw_none_p_kernel(tc, x_words, x_scales, w1, cst, gn, w2, re
                 turn_back(backs[b], part, region == SUM, region == LINEAR)
             return backs
 
-        def finish(first, backs, z_codes):
+        def finish(first, backs, z_codes, tags):
             width = len(backs) * BLOCK
             cols = slice(first * BLOCK, first * BLOCK + width)
             z_bf = work.tile([P, width * PACK], BF16, name="z_bf", align_bytes=64)
@@ -189,9 +189,9 @@ def tile_picked_softdtw_none_p_kernel(tc, x_words, x_scales, w1, cst, gn, w2, re
                 )
             z_bytes = work.tile([P, width], U8, name="z_bytes", align_bytes=64)
             nc.vector.quantize_mx(out=z_codes[:].bitcast(FP8X4), scales=z_bytes[:], in_=z_bf[:])
-            per_bank = BANK // width
+            per_bank = N // P // len(tags)
             for m0 in range(0, N // P, per_bank):
-                acc = psum.tile([P, per_bank, width], F32, name="acc", tag=f"acc{(first + m0 // per_bank) % 2}")
+                acc = psum.tile([P, per_bank, width], F32, name="acc", tag=tags[m0 // per_bank])
                 for m in range(m0, m0 + per_bank):
                     nc.tensor.matmul_mx(
                         out=acc[:, m - m0, :],
@@ -210,7 +210,7 @@ def tile_picked_softdtw_none_p_kernel(tc, x_words, x_scales, w1, cst, gn, w2, re
         second = look_up(1)
         w2_codes = keep.tile([P, N], U32, name="w2_codes", tag="pair0", align_bytes=64)
         nc.vector.quantize_mx(out=w2_codes[:].bitcast(FP8X4), scales=w2_bytes[:], in_=w2_bf[:])
-        finish(0, first, keep.tile([P, CHUNK], U32, name="z_codes", tag="q", align_bytes=64))
+        finish(0, first, keep.tile([P, CHUNK], U32, name="z_codes", tag="q", align_bytes=64), ("acc0", "acc1"))
         last = logarithms(second, ((SUM, 0), (LINEAR, 0), (SUM, 1), (LINEAR, 1)))
         for b, back in enumerate(last):
-            finish(2 + b, [back], work.tile([P, BLOCK], U32, name="z_codes_block", align_bytes=64))
+            finish(2 + b, [back], work.tile([P, BLOCK], U32, name="z_codes_block", align_bytes=64), (("turned0",), ("turned1", "turned2"))[b])

@@ -21,7 +21,7 @@ PACK = 4
 BLOCK = 128
 CHUNK = 256
 HALF = S // 2
-CAP = 32.0
+CAP = 20.0
 SUM, LINEAR = 0, 1
 W1_SPLIT = 52
 
@@ -140,7 +140,8 @@ def tile_picked_softdtw_none_p_kernel(tc, x_words, x_scales, w1, cst, gn, w2, re
             pairs = [[psum.tile([P, 2 * HALF], F32, name="turned", tag=f"turned{2 * b + u}") for u in range(2)] for b in blocks]
             for b in blocks:
                 turn(pairs[b], LINEAR, cst_sb, c * CHUNK + b * BLOCK, True, False)
-                turn(pairs[b], LINEAR, m1, b * BLOCK, False, False)
+                if c == 0:
+                    turn(pairs[b], LINEAR, m1, b * BLOCK, False, False)
             for b in blocks:
                 turn(pairs[b], SUM, e1[b], 0, False, False)
             for t in range(PACK):
@@ -150,15 +151,22 @@ def tile_picked_softdtw_none_p_kernel(tc, x_words, x_scales, w1, cst, gn, w2, re
             e2 = [keep.tile([P, PACK, BLOCK], F32, name=f"e2_{b}", tag=f"late{b}", align_bytes=64) for b in blocks]
             for b in blocks:
                 nc.scalar.activation(e2[b][:], q[:, :, b * BLOCK : (b + 1) * BLOCK], ACT.Exp)
-            for half in ((0, 1), (2, 3)):
+            if c == 0:
+                for half in ((0, 1), (2, 3)):
+                    for b in blocks:
+                        turn(pairs[b], LINEAR, d2, b * BLOCK, False, False, half)
                 for b in blocks:
-                    turn(pairs[b], LINEAR, d2, b * BLOCK, False, False, half)
-            for b in blocks:
-                turn(pairs[b], LINEAR, q, b * BLOCK, False, False)
-                turn(pairs[b], SUM, e2[b], 0, False, True)
+                    turn(pairs[b], LINEAR, q, b * BLOCK, False, False)
+                    turn(pairs[b], SUM, e2[b], 0, False, True)
+            else:
+                for b in blocks:
+                    m2 = work.tile([P, PACK, BLOCK], F32, name="m2")
+                    nc.vector.scalar_tensor_tensor(m2[:], d2[:, :, b * BLOCK : (b + 1) * BLOCK], -CAP, m1[:, :, b * BLOCK : (b + 1) * BLOCK], ALU.min, ALU.add)
+                    turn(pairs[b], SUM, e2[b], 0, False, False)
+                    turn(pairs[b], LINEAR, m2, 0, False, True)
             return pairs
 
-        def logarithms(pairs, steps):
+        def logarithms(pairs, steps, shift):
             backs = [psum.tile([P, PACK * P], F32, name="back", tag=f"back{b}") for b in range(len(pairs))]
             for region, b in steps:
                 if region == SUM:
@@ -170,7 +178,7 @@ def tile_picked_softdtw_none_p_kernel(tc, x_words, x_scales, w1, cst, gn, w2, re
                     if region == SUM:
                         nc.scalar.activation(part[:, u * HALF : (u + 1) * HALF], src, ACT.Ln, bias=1.0)
                     else:
-                        nc.scalar.activation(part[:, u * HALF : (u + 1) * HALF], src, ACT.Copy, scale=-1.0)
+                        nc.scalar.activation(part[:, u * HALF : (u + 1) * HALF], src, ACT.Copy, bias=shift, scale=-1.0)
                 turn_back(backs[b], part, region == SUM, region == LINEAR)
             return backs
 
@@ -206,11 +214,11 @@ def tile_picked_softdtw_none_p_kernel(tc, x_words, x_scales, w1, cst, gn, w2, re
                 nc.vector.tensor_tensor(total[:], acc[:], res_sb[:, m0 : m0 + per_bank, cols], ALU.add)
                 nc.sync.dma_start(out.rearrange("(m p) j -> p m j", p=P)[:, m0 : m0 + per_bank, cols], total[:])
 
-        first = logarithms(look_up(0), ((SUM, 0), (SUM, 1), (LINEAR, 0), (LINEAR, 1)))
+        first = logarithms(look_up(0), ((SUM, 0), (SUM, 1), (LINEAR, 0), (LINEAR, 1)), 0.0)
         second = look_up(1)
         w2_codes = keep.tile([P, N], U32, name="w2_codes", tag="pair0", align_bytes=64)
         nc.vector.quantize_mx(out=w2_codes[:].bitcast(FP8X4), scales=w2_bytes[:], in_=w2_bf[:])
         finish(0, first, keep.tile([P, CHUNK], U32, name="z_codes", tag="q", align_bytes=64), ("acc0", "acc1"))
-        last = logarithms(second, ((SUM, 0), (LINEAR, 0), (SUM, 1), (LINEAR, 1)))
+        last = logarithms(second, ((SUM, 0), (LINEAR, 0), (SUM, 1), (LINEAR, 1)), -CAP)
         for b, back in enumerate(last):
             finish(2 + b, [back], work.tile([P, BLOCK], U32, name="z_codes_block", align_bytes=64), (("turned0",), ("turned1", "turned2"))[b])

from contextlib import ExitStack

import concourse.mybir as mybir
from concourse.masks import make_identity

K, T, S, H, N = 512, 2048, 512, 512, 512
FLOPS = 2 * K * H * S + 2 * H * N * S

F32 = mybir.dt.float32
BF16 = mybir.dt.bfloat16
I32 = mybir.dt.int32
U32 = mybir.dt.uint32
U16 = mybir.dt.uint16
U8 = mybir.dt.uint8
FP8X4 = mybir.dt.float8_e4m3fn_x4
ALU = mybir.AluOpType
ACT = mybir.ActivationFunctionType

P = 128
PACK = 4
BLOCK = 128
CHUNK = 256
HALF = S // 2
CAP = 20.0
SUM, LINEAR = 0, 1
W1_SPLIT = 52


def tile_picked_softdtw_none_p_kernel(tc, x_words, x_scales, w1, cst, gn, w2, res, offs, di, dj, dk, out):
    nc = tc.nc
    with ExitStack() as ctx:
        keep = ctx.enter_context(tc.tile_pool(name="keep", bufs=1))
        work = ctx.enter_context(tc.tile_pool(name="work", bufs=2))
        stores = ctx.enter_context(tc.tile_pool(name="stores", bufs=4))
        psum = ctx.enter_context(tc.psum_pool(name="psum", bufs=1))

        offs_sb = keep.tile([P, S // 16], U16, name="offs_sb")
        di_sb = keep.tile([P, S // 16], U16, name="di_sb")
        dj_sb = keep.tile([P, S // 16], U16, name="dj_sb")
        dk_sb = keep.tile([P, S // 16], U16, name="dk_sb")
        w1_raw = keep.tile([P, PACK, H], F32, name="w1_raw")
        w2_raw = [keep.tile([P, PACK, N // 2], F32, name="w2_raw", tag=f"late{h}", align_bytes=64) for h in range(2)]
        words = keep.tile([P, T], I32, name="words", align_bytes=64)
        scales = keep.tile([P, T], U8, name="scales", align_bytes=64)
        cst_sb = keep.tile([P, PACK, S], F32, name="cst_sb")
        res_sb = keep.tile([P, N // P, S], F32, name="res_sb")
        gn_sb = keep.tile([P, PACK], F32, name="gn_sb")
        ident = keep.tile([P, P], F32, name="ident")

        nc.gpsimd.memset(scales[:].bitcast(I32), 0)
        nc.sync.dma_start(offs_sb[:], offs)
        nc.sync.dma_start(w1_raw[:], w1.rearrange("(p j) c -> p j c", j=PACK))
        for q in range(4):
            nc.sync.dma_start(scales[32 * q : 32 * q + 4, :].bitcast(I32), x_scales[0, 4 * q : 4 * q + 4, :].bitcast(I32))
        nc.sync.dma_start(words[:], x_words[0].rearrange("p n t -> p (n t)").bitcast(I32))
        nc.sync.dma_start(di_sb[:], di)
        nc.sync.dma_start(dj_sb[:], dj)
        nc.sync.dma_start(dk_sb[:], dk)
        for h in range(2):
            nc.sync.dma_start(w2_raw[h][:], w2.rearrange("(p j) c -> p j c", j=PACK)[:, :, h * N // 2 : (h + 1) * N // 2])
        nc.sync.dma_start(cst_sb[:], cst.rearrange("(p t) j -> p t j", t=PACK))
        nc.sync.dma_start(gn_sb[:], gn.rearrange("(p t) o -> p (t o)", t=PACK))
        nc.sync.dma_start(res_sb[:], res.rearrange("(m p) j -> p m j", p=P))
        make_identity(nc, ident[:])

        x_codes = keep.tile([P, S], U32, name="x_codes", align_bytes=64)
        x_bytes = keep.tile([P, S], U8, name="x_bytes", align_bytes=64)
        nc.vector.tensor_copy(x_bytes[:], scales[:].indirect(offs_sb[:]))

        w1_bf = keep.tile([P, PACK * H], BF16, name="w1_bf", align_bytes=64)
        dealt = w1_bf[:].rearrange("p (t m j) -> p m j t", t=PACK, j=PACK)
        source = w1_raw[:].rearrange("p j (m t) -> p m j t", t=PACK)
        nc.vector.tensor_copy(dealt[:, :W1_SPLIT], source[:, :W1_SPLIT])
        nc.scalar.copy(dealt[:, W1_SPLIT:], source[:, W1_SPLIT:])
        w1_codes = keep.tile([P, H], U32, name="w1_codes", tag="weights", align_bytes=64)
        w1_bytes = keep.tile([P, H], U8, name="w1_bytes", align_bytes=64)
        nc.vector.quantize_mx(out=w1_codes[:].bitcast(FP8X4), scales=w1_bytes[:], in_=w1_bf[:])

        y = [keep.tile([P, S], F32, name=f"y{t}") for t in range(PACK)]
        halves = [slice(h * HALF, (h + 1) * HALF) for h in range(2)]
        for h in range(2):
            nc.vector.tensor_copy(x_codes[:, halves[h]], words[:].bitcast(U32).indirect(offs_sb[:, 16 * h : 16 * h + 16]))
        pieces = [(0, halves[0]), (0, halves[1])] + [(t, slice(0, S)) for t in range(1, PACK)]
        for (t, cols), tag in zip(pieces, ("turned0", "turned1", "turned2", "turned3", "back0")):
            bank = psum.tile([P, cols.stop - cols.start], F32, name="y_bank", tag=tag)
            nc.tensor.matmul_mx(
                out=bank[:],
                lhsT=w1_codes[:, t * P : (t + 1) * P].bitcast(FP8X4),
                lhsT_scale=w1_bytes[:, t * P : (t + 1) * P],
                rhs=x_codes[:, cols].bitcast(FP8X4),
                rhs_scale=x_bytes[:, cols],
                start=True,
                stop=True,
            )
            nc.scalar.copy(y[t][:, cols], bank[:])

        w2_bf = keep.tile([P, PACK * N], BF16, name="w2_bf", tag="weights", align_bytes=64)
        for h in range(2):
            nc.scalar.copy(
                w2_bf[:, h * 2 * N : (h + 1) * 2 * N].rearrange("p (c i j) -> p c j i", i=4, j=PACK),
                w2_raw[h][:].rearrange("p j (c i) -> p c j i", i=4),
            )
        w2_bytes = keep.tile([P, N], U8, name="w2_bytes", align_bytes=64)

        def turn(pair, region, src, col0, first, last, tiles=range(PACK)):
            for t in tiles:
                at = region * HALF + (t % 2) * P
                nc.tensor.matmul(
                    pair[t // 2][:, at : at + P], src[:, t, col0 : col0 + BLOCK], ident[:],
                    start=first and t % 2 == 0, stop=last and t % 2 == 1, is_transpose=True,
                )

        def turn_back(bank, src, first, last):
            for t in range(PACK):
                nc.tensor.matmul(
                    bank[:, t * P : (t + 1) * P], src[:, t * P : (t + 1) * P], ident[:],
                    start=first and t == 0, stop=last and t == PACK - 1, is_transpose=True,
                )

        def look_up(c):
            lists = slice(c * CHUNK // 16, (c + 1) * CHUNK // 16)
            blocks = range(CHUNK // BLOCK)
            a = keep.tile([P, PACK, CHUNK], F32, name="a", tag=f"pair{c}", align_bytes=64)
            d1 = keep.tile([P, PACK, CHUNK], F32, name="d1", tag="d1")
            m1 = keep.tile([P, PACK, CHUNK], F32, name="m1", tag=f"pair{1 - c}", align_bytes=64)
            d2 = work.tile([P, PACK, CHUNK], F32, name="d2")
            q = keep.tile([P, PACK, CHUNK], F32, name="q", tag="q", align_bytes=64)
            mag = [keep.tile([P, PACK, BLOCK], F32, name=f"mag{b}", tag=f"late{b}", align_bytes=64) for b in blocks]
            e1 = [work.tile([P, PACK, BLOCK], F32, name=f"e1_{b}") for b in blocks]
            for t in range(PACK):
                nc.vector.tensor_copy(a[:, t, :], y[t][:].indirect(di_sb[:, lists]))
            for t in range(PACK):
                nc.vector.tensor_tensor(d1[:, t, :], y[t][:].indirect(dj_sb[:, lists]), a[:, t, :], ALU.subtract)
            for h in range(2):
                nc.vector.scalar_tensor_tensor(m1[:, 2 * h : 2 * h + 2, :], d1[:, 2 * h : 2 * h + 2, :], 0.0, a[:, 2 * h : 2 * h + 2, :], ALU.min, ALU.add)
            for b in blocks:
                nc.scalar.activation(mag[b][:], d1[:, :, b * BLOCK : (b + 1) * BLOCK], ACT.Abs)
            for b in blocks:
                nc.scalar.activation(e1[b][:], mag[b][:], ACT.Exp, scale=-1.0)
            pairs = [[psum.tile([P, 2 * HALF], F32, name="turned", tag=f"turned{2 * b + u}") for u in range(2)] for b in blocks]
            for b in blocks:
                turn(pairs[b], LINEAR, cst_sb, c * CHUNK + b * BLOCK, True, False)
                if c == 0:
                    turn(pairs[b], LINEAR, m1, b * BLOCK, False, False)
            for b in blocks:
                turn(pairs[b], SUM, e1[b], 0, False, False)
            for t in range(PACK):
                nc.vector.tensor_tensor(d2[:, t, :], y[t][:].indirect(dk_sb[:, lists]), m1[:, t, :], ALU.subtract)
            for b in blocks:
                nc.vector.tensor_scalar(q[:, :, b * BLOCK : (b + 1) * BLOCK], d2[:, :, b * BLOCK : (b + 1) * BLOCK], -CAP, -1.0, ALU.max, ALU.mult)
            e2 = [keep.tile([P, PACK, BLOCK], F32, name=f"e2_{b}", tag=f"late{b}", align_bytes=64) for b in blocks]
            for b in blocks:
                nc.scalar.activation(e2[b][:], q[:, :, b * BLOCK : (b + 1) * BLOCK], ACT.Exp)
            if c == 0:
                for half in ((0, 1), (2, 3)):
                    for b in blocks:
                        turn(pairs[b], LINEAR, d2, b * BLOCK, False, False, half)
                for b in blocks:
                    turn(pairs[b], LINEAR, q, b * BLOCK, False, False)
                    turn(pairs[b], SUM, e2[b], 0, False, True)
            else:
                for b in blocks:
                    m2 = work.tile([P, PACK, BLOCK], F32, name="m2")
                    nc.vector.scalar_tensor_tensor(m2[:], d2[:, :, b * BLOCK : (b + 1) * BLOCK], -CAP, m1[:, :, b * BLOCK : (b + 1) * BLOCK], ALU.min, ALU.add)
                    turn(pairs[b], SUM, e2[b], 0, False, False)
                    turn(pairs[b], LINEAR, m2, 0, False, True)
            return pairs

        def logarithms(pairs, steps, shift):
            backs = [psum.tile([P, PACK * P], F32, name="back", tag=f"back{b}") for b in range(len(pairs))]
            for region, b in steps:
                if region == SUM:
                    part = keep.tile([P, PACK * P], F32, name=f"logs{b}", tag=f"late{b}", align_bytes=64)
                else:
                    part = work.tile([P, PACK * P], F32, name="rest")
                for u in range(2):
                    src = pairs[b][u][:, region * HALF : (region + 1) * HALF]
                    if region == SUM:
                        nc.scalar.activation(part[:, u * HALF : (u + 1) * HALF], src, ACT.Ln, bias=1.0)
                    else:
                        nc.scalar.activation(part[:, u * HALF : (u + 1) * HALF], src, ACT.Copy, bias=shift, scale=-1.0)
                turn_back(backs[b], part, region == SUM, region == LINEAR)
            return backs

        def finish(first, backs, z_codes, tags):
            width = len(backs) * BLOCK
            cols = slice(first * BLOCK, first * BLOCK + width)
            z_bf = work.tile([P, width * PACK], BF16, name="z_bf", align_bytes=64)
            for b, back in enumerate(backs):
                nc.vector.scalar_tensor_tensor(
                    z_bf[:, b * BLOCK * PACK : (b + 1) * BLOCK * PACK].rearrange("p (j t) -> p j t", t=PACK),
                    back[:].rearrange("p (t j) -> p j t", t=PACK),
                    -1.0,
                    gn_sb[:].unsqueeze(1).to_broadcast([P, BLOCK, PACK]),
                    ALU.mult,
                    ALU.mult,
                )
            z_bytes = work.tile([P, width], U8, name="z_bytes", align_bytes=64)
            nc.vector.quantize_mx(out=z_codes[:].bitcast(FP8X4), scales=z_bytes[:], in_=z_bf[:])
            per_bank = N // P // len(tags)
            for m0 in range(0, N // P, per_bank):
                acc = psum.tile([P, per_bank, width], F32, name="acc", tag=tags[m0 // per_bank])
                for m in range(m0, m0 + per_bank):
                    nc.tensor.matmul_mx(
                        out=acc[:, m - m0, :],
                        lhsT=w2_codes[:, m * P : (m + 1) * P].bitcast(FP8X4),
                        lhsT_scale=w2_bytes[:, m * P : (m + 1) * P],
                        rhs=z_codes[:].bitcast(FP8X4),
                        rhs_scale=z_bytes[:],
                        start=True,
                        stop=True,
                    )
                total = stores.tile([P, per_bank, width], F32, name="total")
                nc.vector.tensor_tensor(total[:], acc[:], res_sb[:, m0 : m0 + per_bank, cols], ALU.add)
                nc.sync.dma_start(out.rearrange("(m p) j -> p m j", p=P)[:, m0 : m0 + per_bank, cols], total[:])

        first = logarithms(look_up(0), ((SUM, 0), (SUM, 1), (LINEAR, 0), (LINEAR, 1)), 0.0)
        second = look_up(1)
        w2_codes = keep.tile([P, N], U32, name="w2_codes", tag="pair0", align_bytes=64)
        nc.vector.quantize_mx(out=w2_codes[:].bitcast(FP8X4), scales=w2_bytes[:], in_=w2_bf[:])
        finish(0, first, keep.tile([P, CHUNK], U32, name="z_codes", tag="q", align_bytes=64), ("acc0", "acc1"))
        last = logarithms(second, ((SUM, 0), (LINEAR, 0), (SUM, 1), (LINEAR, 1)), -CAP)
        for b, back in enumerate(last):
            finish(2 + b, [back], work.tile([P, BLOCK], U32, name="z_codes_block", align_bytes=64), (("turned0",), ("turned1", "turned2"))[b])
